import numpy as np
import ml_dtypes


def mxq(x, axis, fmt="e4m3"):
    dtype, down = {"e4m3": (ml_dtypes.float8_e4m3fn, 7), "e5m2": (ml_dtypes.float8_e5m2, 14)}[fmt]
    v = np.moveaxis(np.asarray(x, np.float32).astype(ml_dtypes.bfloat16).astype(np.float64), axis, -1)
    blocks = v.reshape(v.shape[:-1] + (-1, 32))
    amax = np.abs(blocks).max(-1, keepdims=True)
    byte = np.maximum(np.where(amax > 0, np.frexp(amax)[1] - 1 + 127, 0) - down, 1)
    scale = np.exp2(byte - 127.0)
    codes = (blocks / scale).astype(np.float32).astype(dtype).astype(np.float64)
    return np.moveaxis((codes * scale).reshape(v.shape), -1, axis)


WIDE = False


def mx_kscale(k):
    if not WIDE:
        return np.ones(k)
    levels = np.array([10, -10, 5, -5, 0])
    if k % 512:
        return np.exp2(np.random.permutation(np.resize(levels, k // 32))).repeat(32)
    a = np.empty((k // 512, 16))
    for p in range(k // 512):
        a[p, :8] = np.random.permutation(np.resize(levels, 8))
        for g in range(8):
            far = levels[np.abs(levels - a[p, g]) >= 10]
            a[p, g + 8] = far[np.random.randint(len(far))]
    return np.exp2(a.ravel()).repeat(32)


def f64(x):
    return np.asarray(x).astype(np.float64)


E2M1 = np.array([0.0, 0.5, 1.0, 1.5, 2.0, 3.0, 4.0, 6.0, -0.0, -0.5, -1.0, -1.5, -2.0, -3.0, -4.0, -6.0])


def pack_weight(w, fmt):
    k, n = w.shape
    w = f64(np.asarray(w, np.float32).astype(ml_dtypes.bfloat16)).reshape(k // 32, 32, n)
    amax = np.abs(w).max(1)
    if fmt == "e4m3":
        byte = np.frexp(amax)[1] - 1 + 127 - 7
    else:
        mant, ex = np.frexp(amax / 6.0)
        byte = np.where(mant > 0.5, ex, ex - 1) + 127
    byte = np.clip(np.where(amax > 0, byte, 1), 1, 254)
    scaled = (w * np.exp2(127.0 - byte)[:, None, :]).reshape(k, n).astype(np.float32)
    by_word = np.ascontiguousarray(scaled.reshape(k // 512, 128, 4, n).transpose(0, 1, 3, 2))
    if fmt == "e4m3":
        words = by_word.astype(ml_dtypes.float8_e4m3fn).view(np.uint8)
    else:
        c = by_word.astype(ml_dtypes.float4_e2m1fn).view(np.uint8) & 0xF
        words = (c[..., 0::2] | (c[..., 1::2] << 4)).reshape(k // 512, 128, 2 * n)
    return np.ascontiguousarray(words), np.ascontiguousarray(byte.astype(np.uint8).reshape(k // 512, 16, n))


def unpack_weight(words, scales, fmt):
    g, _, n = scales.shape
    words = np.ascontiguousarray(words).reshape(g, 128, n, -1)
    if fmt == "e4m3":
        vals = words.view(ml_dtypes.float8_e4m3fn).astype(np.float64)
    else:
        nib = np.empty((g, 128, n, 4), np.uint8)
        nib[..., 0::2] = words & 0xF
        nib[..., 1::2] = words >> 4
        vals = E2M1[nib]
    vals = vals * np.repeat(np.exp2(scales.astype(np.float64) - 127.0), 8, axis=1)[..., None]
    return vals.transpose(0, 1, 3, 2).reshape(g * 512, n)


K, L, T, N = 512, 1024, 512, 512


def setup_inputs():
    n = np.random.standard_normal
    fk = mx_kscale(K)
    fl = mx_kscale(L)
    xtp = pack_weight(n((K, T)) / fk[:, None], "e4m3")
    wap = pack_weight(n((K, N)) * 1 / np.sqrt(K) * fk[:, None], "e2m1")
    wqp = pack_weight(n((L, N)) * 1 / np.sqrt(L) * fl[:, None], "e2m1")
    wbp = pack_weight(n((K, N)) * 1 / np.sqrt(K) * fk[:, None], "e4m3")
    wsp = pack_weight(n((L, N)) * 1 / np.sqrt(L) * fl[:, None], "e2m1")
    return {
        "xt_words": xtp[0],
        "xt_scales": xtp[1],
        "wa_words": wap[0],
        "wa_scales": wap[1],
        "xq": (n((L, T)) / fl[:, None]).astype(np.float32),
        "wq_words": wqp[0],
        "wq_scales": wqp[1],
        "wb_words": wbp[0],
        "wb_scales": wbp[1],
        "ws_words": wsp[0],
        "ws_scales": wsp[1],
    }


def reference(xt_words, xt_scales, wa_words, wa_scales, xq, wq_words, wq_scales, wb_words, wb_scales, ws_words, ws_scales):
    xtu = unpack_weight(xt_words, xt_scales, "e4m3")
    wau = unpack_weight(wa_words, wa_scales, "e2m1")
    wqu = unpack_weight(wq_words, wq_scales, "e2m1")
    wbu = unpack_weight(wb_words, wb_scales, "e4m3")
    wsu = unpack_weight(ws_words, ws_scales, "e2m1")
    xqq = mxq(f64(xq), 0, "e4m3")
    p = wau.T @ xtu + wqu.T @ xqq
    r = wbu.T @ xtu + wsu.T @ xqq
    d = np.abs(p - r)
    y = np.maximum(p, r) + np.log(1.0 + np.exp(0.0 - d))
    return y

@@ -1,0 +1,194 @@
+from contextlib import ExitStack
+
+import concourse.mybir as mybir
+
+K, L, T, N = 512, 1024, 512, 512
+FLOPS = 2 * 2 * (K + L) * T * N
+
+F32 = mybir.dt.float32
+BF16 = mybir.dt.bfloat16
+U32 = mybir.dt.uint32
+I32 = mybir.dt.int32
+U8 = mybir.dt.uint8
+FP8X4 = mybir.dt.float8_e4m3fn_x4
+FP4X4 = mybir.dt.float4_e2m1fn_x4
+ALU = mybir.AluOpType
+ACT = mybir.ActivationFunctionType
+
+P = 128
+TILES = N // P
+HALF = T // 2
+GAP_LIMIT = 30.0
+
+
+def tile_mix_smooth_larger_of_sums_kernel(
+    tc, xt_words, xt_scales, wa_words, wa_scales, xq, wq_words, wq_scales,
+    wb_words, wb_scales, ws_words, ws_scales, out,
+):
+    nc = tc.nc
+    with ExitStack() as ctx:
+        sb = ctx.enter_context(tc.tile_pool(name="sb", bufs=1))
+        ps = ctx.enter_context(tc.psum_pool(name="ps", bufs=1))
+        ctx.enter_context(tc.manual_schedule())
+
+        def sbt(name, shape, dtype):
+            return sb.tile(shape, dtype, name=name, align_bytes=64)
+
+        xt_c = sbt("xt_c", [P, T], U32)
+        wb_c = sbt("wb_c", [P, N], U32)
+        wa_c = sbt("wa_c", [P, 2 * N], U8)
+        wq_c = sbt("wq_c", [P, 2, 2 * N], U8)
+        ws_c = sbt("ws_c", [P, 2, 2 * N], U8)
+        xt_s = sbt("xt_s", [P, 1, T], U8)
+        wa_s = sbt("wa_s", [P, 1, N], U8)
+        wb_s = sbt("wb_s", [P, 1, N], U8)
+        wq_s = sbt("wq_s", [P, 2, N], U8)
+        ws_s = sbt("ws_s", [P, 2, N], U8)
+        xq_c = [sbt("xq_c%d" % z, [P, T], U32) for z in range(2)]
+        xq_s = [sbt("xq_s%d" % z, [P, T], U8) for z in range(2)]
+        raw0 = sbt("raw0", [P, 4, T], F32)
+        raw1 = [sbt("raw1_%d" % h, [P, 4, HALF], F32) for h in range(2)]
+        grouped = [[sbt("grp%d_%d" % (z, h), [P, HALF, 4], BF16) for h in range(2)] for z in range(2)]
+        zero = sbt("zero", [P, 1], F32)
+        one = sbt("one", [P, 1], F32)
+        p_sb = [sbt("p_sb%d" % j, [P, T], F32) for j in range(TILES)]
+        gap = [sbt("gap%d" % j, [P, T], F32) for j in range(TILES)]
+        gapc = [sbt("gapc%d" % j, [P, T], F32) for j in range(TILES)]
+        ex = [sbt("ex%d" % j, [P, T], F32) for j in range(TILES)]
+        base = [sbt("base%d" % j, [P, T], F32) for j in range(TILES)]
+        lg = [sbt("lg%d" % j, [P, T], F32) for j in range(TILES)]
+        res = [sbt("res%d" % j, [P, T], F32) for j in range(TILES)]
+        p_ps = [ps.tile([P, T], F32, name="p_ps%d" % j) for j in range(TILES)]
+        r_ps = [ps.tile([P, T], F32, name="r_ps%d" % j) for j in range(TILES)]
+
+        def clear(plane):
+            nc.vector.memset(plane[:].rearrange("p z c -> p (z c)").bitcast(I32), 0)
+
+        def load_scales(eng, plane, src, r):
+            eng.dma_start(
+                out=plane[r:P:32, :, :].bitcast(I32),
+                in_=src.rearrange("z (q r) c -> r q z c", r=4)[r].bitcast(I32),
+            )
+
+        def load_words(dst, src):
+            nc.sync.dma_start(out=dst[:].bitcast(I32), in_=src.bitcast(I32))
+
+        nc.vector.memset(zero[:], 0.0)
+        for plane in (xt_s, wb_s, wa_s, wq_s, ws_s):
+            clear(plane)
+        nc.scalar.activation(out=one[:], in_=zero[:], func=ACT.Exp)
+
+        for r in range(4):
+            load_scales(nc.gpsimd, wb_s, wb_scales, r)
+
+        rows = [xq[K * z : K * (z + 1), :].rearrange("(p j) t -> p j t", j=4) for z in range(2)]
+        load_words(xt_c, xt_words[0].rearrange("p n t -> p (n t)"))
+        load_words(wa_c, wa_words[0])
+        for r in range(4):
+            load_scales(nc.sync, xt_s, xt_scales, r)
+        load_scales(nc.sync, wa_s, wa_scales, 0)
+        nc.sync.dma_start(out=raw0[:], in_=rows[0])
+        for r in range(1, 4):
+            load_scales(nc.sync, wa_s, wa_scales, r)
+        load_words(wb_c, wb_words[0].rearrange("p n t -> p (n t)"))
+        load_words(wq_c, wq_words.rearrange("z p c -> p z c"))
+        nc.sync.dma_start(out=raw1[0][:], in_=rows[1][:, :, 0:HALF])
+        for r in range(3):
+            load_scales(nc.sync, wq_s, wq_scales, r)
+        load_scales(nc.sync, wq_s, wq_scales, 3)
+        nc.sync.dma_start(out=raw1[1][:], in_=rows[1][:, :, HALF:T])
+        load_words(ws_c, ws_words.rearrange("z p c -> p z c"))
+        for r in range(4):
+            load_scales(nc.sync, ws_s, ws_scales, r)
+
+        def views(src, s0, dst, d0, n):
+            return (
+                dst[:, d0 : d0 + n, :].rearrange("p (c i) j -> p c j i", i=4),
+                src[:, :, s0 : s0 + n].rearrange("p j (c i) -> p c j i", i=4),
+            )
+
+        def cast_v(src, s0, dst, d0, n):
+            o, i = views(src, s0, dst, d0, n)
+            nc.vector.tensor_copy(out=o, in_=i)
+
+        def cast_s(src, s0, dst, d0, n):
+            o, i = views(src, s0, dst, d0, n)
+            nc.scalar.copy(out=o, in_=i)
+
+        def quantize(z, h):
+            cols = slice(HALF * h, HALF * (h + 1))
+            nc.vector.quantize_mx(
+                out=xq_c[z][:, cols].bitcast(FP8X4),
+                scales=xq_s[z][:, cols],
+                in_=grouped[z][h][:].rearrange("p t j -> p (t j)"),
+            )
+
+        cast_v(raw0, 0, grouped[0][0], 0, HALF)
+        cast_s(raw0, HALF + 64, grouped[0][1], 64, HALF - 64)
+        cast_v(raw0, HALF, grouped[0][1], 0, 64)
+        quantize(0, 0)
+        quantize(0, 1)
+        for h in range(2):
+            cast_v(raw1[h], 0, grouped[1][h], 0, 160)
+            cast_s(raw1[h], 160, grouped[1][h], 160, HALF - 160)
+            quantize(1, h)
+
+        def mm(acc, w_c, fp4, w_s, z, j, x_c, x_s, start, stop):
+            if fp4:
+                lhsT = w_c[:, 2 * P * j : 2 * P * (j + 1)].bitcast(FP4X4)
+            else:
+                lhsT = w_c[:, P * j : P * (j + 1)].bitcast(FP8X4)
+            nc.tensor.matmul_mx(
+                out=acc[:], lhsT=lhsT, lhsT_scale=w_s[:, z, P * j : P * (j + 1)],
+                rhs=x_c[:].bitcast(FP8X4), rhs_scale=x_s, start=start, stop=stop,
+            )
+
+        for j in range(TILES):
+            mm(p_ps[j], wa_c[:], True, wa_s, 0, j, xt_c, xt_s[:, 0, :], True, False)
+        for j in range(TILES):
+            mm(r_ps[j], wb_c[:], False, wb_s, 0, j, xt_c, xt_s[:, 0, :], True, False)
+        for j in range(TILES):
+            mm(p_ps[j], wq_c[:, 0, :], True, wq_s, 0, j, xq_c[0], xq_s[0][:], False, False)
+        for j in range(TILES):
+            mm(p_ps[j], wq_c[:, 1, :], True, wq_s, 1, j, xq_c[1], xq_s[1][:], False, True)
+            mm(r_ps[j], ws_c[:, 0, :], True, ws_s, 0, j, xq_c[0], xq_s[0][:], False, False)
+            mm(r_ps[j], ws_c[:, 1, :], True, ws_s, 1, j, xq_c[1], xq_s[1][:], False, True)
+
+        def leave(j):
+            nc.scalar.copy(out=p_sb[j][:], in_=p_ps[j][:])
+
+        def diff(j, a, b):
+            nc.vector.tensor_tensor(out=gap[j][:, a:b], in0=p_sb[j][:, a:b], in1=r_ps[j][:, a:b], op=ALU.subtract)
+
+        def clamp(j, a, b):
+            nc.vector.tensor_scalar(
+                out=gapc[j][:, a:b], in0=gap[j][:, a:b], scalar1=-GAP_LIMIT, scalar2=None, op0=ALU.max
+            )
+
+        def expo(j, a, b):
+            nc.scalar.activation(out=ex[j][:, a:b], in_=gapc[j][:, a:b], func=ACT.Exp, scale=-1.0)
+
+        leave(0)
+        leave(1)
+        for j in range(TILES):
+            diff(j, 0, HALF)
+            diff(j, HALF, T)
+            clamp(j, 0, HALF)
+            clamp(j, HALF, T)
+            if j + 2 < TILES:
+                leave(j + 2)
+            if j + 1 < TILES:
+                expo(j, 0, T)
+            else:
+                expo(j, 0, HALF)
+                expo(j, HALF, T)
+        for j in range(TILES):
+            nc.vector.scalar_tensor_tensor(
+                out=base[j][:], in0=r_ps[j][:], scalar=-GAP_LIMIT, in1=p_sb[j][:], op0=ALU.add, op1=ALU.max
+            )
+
+        pieces = [(0, 0, HALF), (0, HALF, T), (1, 0, T), (2, 0, T), (3, 0, 384), (3, 384, T)]
+        for j, a, b in pieces:
+            nc.scalar.activation(out=lg[j][:, a:b], in_=ex[j][:, a:b], func=ACT.Ln, bias=one[:])
+            nc.vector.tensor_tensor(out=res[j][:, a:b], in0=base[j][:, a:b], in1=lg[j][:, a:b], op=ALU.add)
+            nc.sync.dma_start(out=out[P * j : P * (j + 1), a:b], in_=res[j][:, a:b])

@@ -1,3 +1,4 @@
+import math
 from contextlib import ExitStack
 
 import concourse.mybir as mybir
@@ -18,7 +19,9 @@ ACT = mybir.ActivationFunctionType
 P = 128
 TILES = N // P
 HALF = T // 2
-GAP_LIMIT = 30.0
+GAP_LIMIT = 20.0
+LOG_FLOOR = -GAP_LIMIT - math.log(1.0 + math.exp(-GAP_LIMIT))
+TINY = 2.0 ** -60
 
 
 def tile_mix_smooth_larger_of_sums_kernel(
@@ -39,67 +42,56 @@ def tile_mix_smooth_larger_of_sums_kernel(
         wa_c = sbt("wa_c", [P, 2 * N], U8)
         wq_c = sbt("wq_c", [P, 2, 2 * N], U8)
         ws_c = sbt("ws_c", [P, 2, 2 * N], U8)
-        xt_s = sbt("xt_s", [P, 1, T], U8)
-        wa_s = sbt("wa_s", [P, 1, N], U8)
-        wb_s = sbt("wb_s", [P, 1, N], U8)
-        wq_s = sbt("wq_s", [P, 2, N], U8)
-        ws_s = sbt("ws_s", [P, 2, N], U8)
+        staged = sbt("staged", [16, 7, N], U8)
+        planes = sbt("planes", [P, 7, N], U8)
+        xt_s, wa_s, wb_s = planes[:, 0:1, :], planes[:, 1:2, :], planes[:, 2:3, :]
+        wq_s, ws_s = planes[:, 3:5, :], planes[:, 5:7, :]
         xq_c = [sbt("xq_c%d" % z, [P, T], U32) for z in range(2)]
         xq_s = [sbt("xq_s%d" % z, [P, T], U8) for z in range(2)]
         raw0 = sbt("raw0", [P, 4, T], F32)
         raw1 = [sbt("raw1_%d" % h, [P, 4, HALF], F32) for h in range(2)]
         grouped = [[sbt("grp%d_%d" % (z, h), [P, HALF, 4], BF16) for h in range(2)] for z in range(2)]
         zero = sbt("zero", [P, 1], F32)
-        one = sbt("one", [P, 1], F32)
+        tiny = sbt("tiny", [P, 1], F32)
+        half = sbt("half", [P, 1], F32)
         p_sb = [sbt("p_sb%d" % j, [P, T], F32) for j in range(TILES)]
         gap = [sbt("gap%d" % j, [P, T], F32) for j in range(TILES)]
-        gapc = [sbt("gapc%d" % j, [P, T], F32) for j in range(TILES)]
-        ex = [sbt("ex%d" % j, [P, T], F32) for j in range(TILES)]
+        sig = [sbt("sig%d" % j, [P, T], F32) for j in range(TILES)]
         base = [sbt("base%d" % j, [P, T], F32) for j in range(TILES)]
         lg = [sbt("lg%d" % j, [P, T], F32) for j in range(TILES)]
         res = [sbt("res%d" % j, [P, T], F32) for j in range(TILES)]
         p_ps = [ps.tile([P, T], F32, name="p_ps%d" % j) for j in range(TILES)]
         r_ps = [ps.tile([P, T], F32, name="r_ps%d" % j) for j in range(TILES)]
 
-        def clear(plane):
-            nc.vector.memset(plane[:].rearrange("p z c -> p (z c)").bitcast(I32), 0)
-
-        def load_scales(eng, plane, src, r):
-            eng.dma_start(
-                out=plane[r:P:32, :, :].bitcast(I32),
-                in_=src.rearrange("z (q r) c -> r q z c", r=4)[r].bitcast(I32),
-            )
-
         def load_words(dst, src):
             nc.sync.dma_start(out=dst[:].bitcast(I32), in_=src.bitcast(I32))
 
         nc.vector.memset(zero[:], 0.0)
-        for plane in (xt_s, wb_s, wa_s, wq_s, ws_s):
-            clear(plane)
-        nc.scalar.activation(out=one[:], in_=zero[:], func=ACT.Exp)
-
-        for r in range(4):
-            load_scales(nc.gpsimd, wb_s, wb_scales, r)
+        flat = planes[:].rearrange("p z c -> p (z c)").bitcast(I32)
+        nc.vector.memset(flat, 0)
 
         rows = [xq[K * z : K * (z + 1), :].rearrange("(p j) t -> p j t", j=4) for z in range(2)]
         load_words(xt_c, xt_words[0].rearrange("p n t -> p (n t)"))
         load_words(wa_c, wa_words[0])
-        for r in range(4):
-            load_scales(nc.sync, xt_s, xt_scales, r)
-        load_scales(nc.sync, wa_s, wa_scales, 0)
-        nc.sync.dma_start(out=raw0[:], in_=rows[0])
-        for r in range(1, 4):
-            load_scales(nc.sync, wa_s, wa_scales, r)
+        slot = 0
+        for src in (xt_scales, wa_scales, wb_scales, wq_scales, ws_scales):
+            passes = src.shape[0]
+            nc.scalar.dma_start(
+                out=staged[:, slot : slot + passes, :].bitcast(I32),
+                in_=src.rearrange("z q c -> q z c").bitcast(I32),
+            )
+            slot = slot + passes
+        nc.scalar.dma_start(out=raw0[:], in_=rows[0])
+        nc.scalar.activation(out=half[:], in_=zero[:], func=ACT.Sigmoid)
+        nc.vector.tensor_scalar(out=tiny[:], in0=half[:], scalar1=2.0 * TINY, scalar2=None, op0=ALU.mult)
+        staged_flat = staged[:].rearrange("p z c -> p (z c)").bitcast(I32)
+        for q in range(4):
+            nc.sync.dma_start(out=flat[32 * q : 32 * q + 4, :], in_=staged_flat[4 * q : 4 * q + 4, :])
         load_words(wb_c, wb_words[0].rearrange("p n t -> p (n t)"))
         load_words(wq_c, wq_words.rearrange("z p c -> p z c"))
         nc.sync.dma_start(out=raw1[0][:], in_=rows[1][:, :, 0:HALF])
-        for r in range(3):
-            load_scales(nc.sync, wq_s, wq_scales, r)
-        load_scales(nc.sync, wq_s, wq_scales, 3)
         nc.sync.dma_start(out=raw1[1][:], in_=rows[1][:, :, HALF:T])
         load_words(ws_c, ws_words.rearrange("z p c -> p z c"))
-        for r in range(4):
-            load_scales(nc.sync, ws_s, ws_scales, r)
 
         def views(src, s0, dst, d0, n):
             return (
@@ -151,44 +143,29 @@ def tile_mix_smooth_larger_of_sums_kernel(
             mm(p_ps[j], wq_c[:, 0, :], True, wq_s, 0, j, xq_c[0], xq_s[0][:], False, False)
         for j in range(TILES):
             mm(p_ps[j], wq_c[:, 1, :], True, wq_s, 1, j, xq_c[1], xq_s[1][:], False, True)
+        for j in range(TILES):
             mm(r_ps[j], ws_c[:, 0, :], True, ws_s, 0, j, xq_c[0], xq_s[0][:], False, False)
             mm(r_ps[j], ws_c[:, 1, :], True, ws_s, 1, j, xq_c[1], xq_s[1][:], False, True)
 
-        def leave(j):
-            nc.scalar.copy(out=p_sb[j][:], in_=p_ps[j][:])
+        for j in range(0, TILES, 2):
+            nc.vector.tensor_copy(out=p_sb[j][:], in_=p_ps[j][:])
+            nc.scalar.copy(out=p_sb[j + 1][:], in_=p_ps[j + 1][:])
 
-        def diff(j, a, b):
-            nc.vector.tensor_tensor(out=gap[j][:, a:b], in0=p_sb[j][:, a:b], in1=r_ps[j][:, a:b], op=ALU.subtract)
-
-        def clamp(j, a, b):
-            nc.vector.tensor_scalar(
-                out=gapc[j][:, a:b], in0=gap[j][:, a:b], scalar1=-GAP_LIMIT, scalar2=None, op0=ALU.max
-            )
-
-        def expo(j, a, b):
-            nc.scalar.activation(out=ex[j][:, a:b], in_=gapc[j][:, a:b], func=ACT.Exp, scale=-1.0)
-
-        leave(0)
-        leave(1)
         for j in range(TILES):
-            diff(j, 0, HALF)
-            diff(j, HALF, T)
-            clamp(j, 0, HALF)
-            clamp(j, HALF, T)
-            if j + 2 < TILES:
-                leave(j + 2)
-            if j + 1 < TILES:
-                expo(j, 0, T)
-            else:
-                expo(j, 0, HALF)
-                expo(j, HALF, T)
+            for h in range(2):
+                cols = slice(HALF * h, HALF * (h + 1))
+                nc.vector.tensor_tensor(out=gap[j][:, cols], in0=p_sb[j][:, cols], in1=r_ps[j][:, cols], op=ALU.subtract)
+                nc.scalar.activation(out=sig[j][:, cols], in_=gap[j][:, cols], func=ACT.Sigmoid)
         for j in range(TILES):
             nc.vector.scalar_tensor_tensor(
                 out=base[j][:], in0=r_ps[j][:], scalar=-GAP_LIMIT, in1=p_sb[j][:], op0=ALU.add, op1=ALU.max
             )
 
-        pieces = [(0, 0, HALF), (0, HALF, T), (1, 0, T), (2, 0, T), (3, 0, 384), (3, 384, T)]
+        pieces = [(0, 0, 128), (0, 128, T), (1, 0, T), (2, 0, T), (3, 0, 384), (3, 384, T)]
         for j, a, b in pieces:
-            nc.scalar.activation(out=lg[j][:, a:b], in_=ex[j][:, a:b], func=ACT.Ln, bias=one[:])
-            nc.vector.tensor_tensor(out=res[j][:, a:b], in0=base[j][:, a:b], in1=lg[j][:, a:b], op=ALU.add)
+            nc.scalar.activation(out=lg[j][:, a:b], in_=sig[j][:, a:b], func=ACT.Ln, bias=tiny[:])
+            nc.vector.scalar_tensor_tensor(
+                out=res[j][:, a:b], in0=lg[j][:, a:b], scalar=LOG_FLOOR, in1=base[j][:, a:b],
+                op0=ALU.max, op1=ALU.subtract, reverse1=True,
+            )
             nc.sync.dma_start(out=out[P * j : P * (j + 1), a:b], in_=res[j][:, a:b])

@@ -42,7 +42,7 @@ def tile_mix_smooth_larger_of_sums_kernel(
         wa_c = sbt("wa_c", [P, 2 * N], U8)
         wq_c = sbt("wq_c", [P, 2, 2 * N], U8)
         ws_c = sbt("ws_c", [P, 2, 2 * N], U8)
-        staged = sbt("staged", [16, 7, N], U8)
+        staged = sbt("staged", [P, 7, N], U8)
         planes = sbt("planes", [P, 7, N], U8)
         xt_s, wa_s, wb_s = planes[:, 0:1, :], planes[:, 1:2, :], planes[:, 2:3, :]
         wq_s, ws_s = planes[:, 3:5, :], planes[:, 5:7, :]
@@ -77,7 +77,7 @@ def tile_mix_smooth_larger_of_sums_kernel(
         for src in (xt_scales, wa_scales, wb_scales, wq_scales, ws_scales):
             passes = src.shape[0]
             nc.scalar.dma_start(
-                out=staged[:, slot : slot + passes, :].bitcast(I32),
+                out=staged[4:P:8, slot : slot + passes, :].bitcast(I32),
                 in_=src.rearrange("z q c -> q z c").bitcast(I32),
             )
             slot = slot + passes
@@ -85,8 +85,8 @@ def tile_mix_smooth_larger_of_sums_kernel(
         nc.scalar.activation(out=half[:], in_=zero[:], func=ACT.Sigmoid)
         nc.vector.tensor_scalar(out=tiny[:], in0=half[:], scalar1=2.0 * TINY, scalar2=None, op0=ALU.mult)
         staged_flat = staged[:].rearrange("p z c -> p (z c)").bitcast(I32)
-        for q in range(4):
-            nc.sync.dma_start(out=flat[32 * q : 32 * q + 4, :], in_=staged_flat[4 * q : 4 * q + 4, :])
+        for r in range(4):
+            nc.sync.dma_start(out=flat[r:P:32, :], in_=staged_flat[4 + 8 * r : P : 32, :])
         load_words(wb_c, wb_words[0].rearrange("p n t -> p (n t)"))
         load_words(wq_c, wq_words.rearrange("z p c -> p z c"))
         nc.sync.dma_start(out=raw1[0][:], in_=rows[1][:, :, 0:HALF])

@@ -21,6 +21,7 @@ TILES = N // P
 HALF = T // 2
 GAP_LIMIT = 20.0
 LOG_FLOOR = -GAP_LIMIT - math.log(1.0 + math.exp(-GAP_LIMIT))
+WARM = 20
 TINY = 2.0 ** -60
 
 
@@ -40,17 +41,22 @@ def tile_mix_smooth_larger_of_sums_kernel(
         xt_c = sbt("xt_c", [P, T], U32)
         wb_c = sbt("wb_c", [P, N], U32)
         wa_c = sbt("wa_c", [P, 2 * N], U8)
-        wq_c = sbt("wq_c", [P, 2, 2 * N], U8)
+        wq_c = [sbt("wq_c%d" % z, [P, 2 * N], U8) for z in range(2)]
         ws_c = sbt("ws_c", [P, 2, 2 * N], U8)
         staged = sbt("staged", [P, 7, N], U8)
-        planes = sbt("planes", [P, 7, N], U8)
-        xt_s, wa_s, wb_s = planes[:, 0:1, :], planes[:, 1:2, :], planes[:, 2:3, :]
-        wq_s, ws_s = planes[:, 3:5, :], planes[:, 5:7, :]
+        early = sbt("early", [P, 4, N], U8)
+        late = sbt("late", [P, 3, N], U8)
+        xt_s, wa_s, wb_s = early[:, 0, :], early[:, 1, :], early[:, 2, :]
+        wq_s = [early[:, 3, :], late[:, 0, :]]
+        ws_s = [late[:, 1, :], late[:, 2, :]]
         xq_c = [sbt("xq_c%d" % z, [P, T], U32) for z in range(2)]
         xq_s = [sbt("xq_s%d" % z, [P, T], U8) for z in range(2)]
         raw0 = sbt("raw0", [P, 4, T], F32)
         raw1 = [sbt("raw1_%d" % h, [P, 4, HALF], F32) for h in range(2)]
         grouped = [[sbt("grp%d_%d" % (z, h), [P, HALF, 4], BF16) for h in range(2)] for z in range(2)]
+        warm_in = sbt("warm_in", [P, 4 * P], BF16)
+        warm_c = sbt("warm_c", [P, P], U32)
+        warm_s = sbt("warm_s", [P, P], U8)
         zero = sbt("zero", [P, 1], F32)
         tiny = sbt("tiny", [P, 1], F32)
         half = sbt("half", [P, 1], F32)
@@ -67,8 +73,12 @@ def tile_mix_smooth_larger_of_sums_kernel(
             nc.sync.dma_start(out=dst[:].bitcast(I32), in_=src.bitcast(I32))
 
         nc.vector.memset(zero[:], 0.0)
-        flat = planes[:].rearrange("p z c -> p (z c)").bitcast(I32)
-        nc.vector.memset(flat, 0)
+        early_flat = early[:].rearrange("p z c -> p (z c)").bitcast(I32)
+        late_flat = late[:].rearrange("p z c -> p (z c)").bitcast(I32)
+        nc.vector.memset(early_flat, 0)
+        nc.vector.memset(late_flat, 0)
+        nc.vector.memset(warm_in[:], 1.0)
+        nc.vector.quantize_mx(out=warm_c[:].bitcast(FP8X4), scales=warm_s[:], in_=warm_in[:])
 
         rows = [xq[K * z : K * (z + 1), :].rearrange("(p j) t -> p j t", j=4) for z in range(2)]
         load_words(xt_c, xt_words[0].rearrange("p n t -> p (n t)"))
@@ -85,12 +95,19 @@ def tile_mix_smooth_larger_of_sums_kernel(
         nc.scalar.activation(out=half[:], in_=zero[:], func=ACT.Sigmoid)
         nc.vector.tensor_scalar(out=tiny[:], in0=half[:], scalar1=2.0 * TINY, scalar2=None, op0=ALU.mult)
         staged_flat = staged[:].rearrange("p z c -> p (z c)").bitcast(I32)
-        for r in range(4):
-            nc.sync.dma_start(out=flat[r:P:32, :], in_=staged_flat[4 + 8 * r : P : 32, :])
+
+        def place(flat, lo, hi):
+            words = slice(lo * N // 4, hi * N // 4)
+            for r in range(4):
+                nc.sync.dma_start(out=flat[r:P:32, :], in_=staged_flat[4 + 8 * r : P : 32, words])
+
+        place(early_flat, 0, 4)
         load_words(wb_c, wb_words[0].rearrange("p n t -> p (n t)"))
-        load_words(wq_c, wq_words.rearrange("z p c -> p z c"))
+        load_words(wq_c[0], wq_words[0])
         nc.sync.dma_start(out=raw1[0][:], in_=rows[1][:, :, 0:HALF])
         nc.sync.dma_start(out=raw1[1][:], in_=rows[1][:, :, HALF:T])
+        load_words(wq_c[1], wq_words[1])
+        place(late_flat, 4, 7)
         load_words(ws_c, ws_words.rearrange("z p c -> p z c"))
 
         def views(src, s0, dst, d0, n):
@@ -125,27 +142,32 @@ def tile_mix_smooth_larger_of_sums_kernel(
             cast_s(raw1[h], 160, grouped[1][h], 160, HALF - 160)
             quantize(1, h)
 
-        def mm(acc, w_c, fp4, w_s, z, j, x_c, x_s, start, stop):
+        def mm(acc, w_c, fp4, w_s, j, x_c, x_s, start, stop):
             if fp4:
                 lhsT = w_c[:, 2 * P * j : 2 * P * (j + 1)].bitcast(FP4X4)
             else:
                 lhsT = w_c[:, P * j : P * (j + 1)].bitcast(FP8X4)
             nc.tensor.matmul_mx(
-                out=acc[:], lhsT=lhsT, lhsT_scale=w_s[:, z, P * j : P * (j + 1)],
+                out=acc[:], lhsT=lhsT, lhsT_scale=w_s[:, P * j : P * (j + 1)],
                 rhs=x_c[:].bitcast(FP8X4), rhs_scale=x_s, start=start, stop=stop,
             )
 
+        for w in range(WARM):
+            nc.tensor.matmul_mx(
+                out=r_ps[3][:, 0:P], lhsT=warm_c[:].bitcast(FP8X4), lhsT_scale=warm_s[:],
+                rhs=xt_c[:, 0:P].bitcast(FP8X4), rhs_scale=warm_s[:], start=True, stop=True,
+            )
         for j in range(TILES):
-            mm(p_ps[j], wa_c[:], True, wa_s, 0, j, xt_c, xt_s[:, 0, :], True, False)
+            mm(p_ps[j], wa_c[:], True, wa_s, j, xt_c, xt_s, True, False)
         for j in range(TILES):
-            mm(r_ps[j], wb_c[:], False, wb_s, 0, j, xt_c, xt_s[:, 0, :], True, False)
+            mm(r_ps[j], wb_c[:], False, wb_s, j, xt_c, xt_s, True, False)
         for j in range(TILES):
-            mm(p_ps[j], wq_c[:, 0, :], True, wq_s, 0, j, xq_c[0], xq_s[0][:], False, False)
+            mm(p_ps[j], wq_c[0][:], True, wq_s[0], j, xq_c[0], xq_s[0][:], False, False)
         for j in range(TILES):
-            mm(p_ps[j], wq_c[:, 1, :], True, wq_s, 1, j, xq_c[1], xq_s[1][:], False, True)
+            mm(p_ps[j], wq_c[1][:], True, wq_s[1], j, xq_c[1], xq_s[1][:], False, True)
         for j in range(TILES):
-            mm(r_ps[j], ws_c[:, 0, :], True, ws_s, 0, j, xq_c[0], xq_s[0][:], False, False)
-            mm(r_ps[j], ws_c[:, 1, :], True, ws_s, 1, j, xq_c[1], xq_s[1][:], False, True)
+            mm(r_ps[j], ws_c[:, 0, :], True, ws_s[0], j, xq_c[0], xq_s[0][:], False, False)
+            mm(r_ps[j], ws_c[:, 1, :], True, ws_s[1], j, xq_c[1], xq_s[1][:], False, True)
 
         for j in range(0, TILES, 2):
             nc.vector.tensor_copy(out=p_sb[j][:], in_=p_ps[j][:])
@@ -161,11 +183,14 @@ def tile_mix_smooth_larger_of_sums_kernel(
                 out=base[j][:], in0=r_ps[j][:], scalar=-GAP_LIMIT, in1=p_sb[j][:], op0=ALU.add, op1=ALU.max
             )
 
-        pieces = [(0, 0, 128), (0, 128, T), (1, 0, T), (2, 0, T), (3, 0, 384), (3, 384, T)]
-        for j, a, b in pieces:
-            nc.scalar.activation(out=lg[j][:, a:b], in_=sig[j][:, a:b], func=ACT.Ln, bias=tiny[:])
-            nc.vector.scalar_tensor_tensor(
-                out=res[j][:, a:b], in0=lg[j][:, a:b], scalar=LOG_FLOOR, in1=base[j][:, a:b],
-                op0=ALU.max, op1=ALU.subtract, reverse1=True,
-            )
-            nc.sync.dma_start(out=out[P * j : P * (j + 1), a:b], in_=res[j][:, a:b])
+        cuts = [[[0, 128], [128, HALF, T]], [[0, HALF, T]], [[0, HALF, T]], [[0, HALF, 384], [384, T]]]
+        for j in range(TILES):
+            for store in cuts[j]:
+                for a, b in zip(store, store[1:]):
+                    nc.scalar.activation(out=lg[j][:, a:b], in_=sig[j][:, a:b], func=ACT.Ln, bias=tiny[:])
+                    nc.vector.scalar_tensor_tensor(
+                        out=res[j][:, a:b], in0=lg[j][:, a:b], scalar=LOG_FLOOR, in1=base[j][:, a:b],
+                        op0=ALU.max, op1=ALU.subtract, reverse1=True,
+                    )
+                a, b = store[0], store[-1]
+                nc.sync.dma_start(out=out[P * j : P * (j + 1), a:b], in_=res[j][:, a:b])

import math
from contextlib import ExitStack

import concourse.mybir as mybir

K, L, T, N = 512, 1024, 512, 512
FLOPS = 2 * 2 * (K + L) * T * N

F32 = mybir.dt.float32
BF16 = mybir.dt.bfloat16
U32 = mybir.dt.uint32
I32 = mybir.dt.int32
U8 = mybir.dt.uint8
FP8X4 = mybir.dt.float8_e4m3fn_x4
FP4X4 = mybir.dt.float4_e2m1fn_x4
ALU = mybir.AluOpType
ACT = mybir.ActivationFunctionType

P = 128
TILES = N // P
HALF = T // 2
GAP_LIMIT = 20.0
LOG_FLOOR = -GAP_LIMIT - math.log(1.0 + math.exp(-GAP_LIMIT))
WARM = 20
TINY = 2.0 ** -60


def tile_mix_smooth_larger_of_sums_kernel(
    tc, xt_words, xt_scales, wa_words, wa_scales, xq, wq_words, wq_scales,
    wb_words, wb_scales, ws_words, ws_scales, out,
):
    nc = tc.nc
    with ExitStack() as ctx:
        sb = ctx.enter_context(tc.tile_pool(name="sb", bufs=1))
        ps = ctx.enter_context(tc.psum_pool(name="ps", bufs=1))
        ctx.enter_context(tc.manual_schedule())

        def sbt(name, shape, dtype):
            return sb.tile(shape, dtype, name=name, align_bytes=64)

        xt_c = sbt("xt_c", [P, T], U32)
        wb_c = sbt("wb_c", [P, N], U32)
        wa_c = sbt("wa_c", [P, 2 * N], U8)
        wq_c = [sbt("wq_c%d" % z, [P, 2 * N], U8) for z in range(2)]
        ws_c = sbt("ws_c", [P, 2, 2 * N], U8)
        staged = sbt("staged", [P, 7, N], U8)
        early = sbt("early", [P, 4, N], U8)
        late = sbt("late", [P, 3, N], U8)
        xt_s, wa_s, wb_s = early[:, 0, :], early[:, 1, :], early[:, 2, :]
        wq_s = [early[:, 3, :], late[:, 0, :]]
        ws_s = [late[:, 1, :], late[:, 2, :]]
        xq_c = [sbt("xq_c%d" % z, [P, T], U32) for z in range(2)]
        xq_s = [sbt("xq_s%d" % z, [P, T], U8) for z in range(2)]
        raw0 = sbt("raw0", [P, 4, T], F32)
        raw1 = [sbt("raw1_%d" % h, [P, 4, HALF], F32) for h in range(2)]
        grouped = [[sbt("grp%d_%d" % (z, h), [P, HALF, 4], BF16) for h in range(2)] for z in range(2)]
        warm_in = sbt("warm_in", [P, 4 * P], BF16)
        warm_c = sbt("warm_c", [P, P], U32)
        warm_s = sbt("warm_s", [P, P], U8)
        zero = sbt("zero", [P, 1], F32)
        tiny = sbt("tiny", [P, 1], F32)
        half = sbt("half", [P, 1], F32)
        p_sb = [sbt("p_sb%d" % j, [P, T], F32) for j in range(TILES)]
        gap = [sbt("gap%d" % j, [P, T], F32) for j in range(TILES)]
        sig = [sbt("sig%d" % j, [P, T], F32) for j in range(TILES)]
        base = [sbt("base%d" % j, [P, T], F32) for j in range(TILES)]
        lg = [sbt("lg%d" % j, [P, T], F32) for j in range(TILES)]
        res = [sbt("res%d" % j, [P, T], F32) for j in range(TILES)]
        p_ps = [ps.tile([P, T], F32, name="p_ps%d" % j) for j in range(TILES)]
        r_ps = [ps.tile([P, T], F32, name="r_ps%d" % j) for j in range(TILES)]

        def load_words(dst, src):
            nc.sync.dma_start(out=dst[:].bitcast(I32), in_=src.bitcast(I32))

        nc.vector.memset(zero[:], 0.0)
        early_flat = early[:].rearrange("p z c -> p (z c)").bitcast(I32)
        late_flat = late[:].rearrange("p z c -> p (z c)").bitcast(I32)
        nc.vector.memset(early_flat, 0)
        nc.vector.memset(late_flat, 0)
        nc.vector.memset(warm_in[:], 1.0)
        nc.vector.quantize_mx(out=warm_c[:].bitcast(FP8X4), scales=warm_s[:], in_=warm_in[:])

        rows = [xq[K * z : K * (z + 1), :].rearrange("(p j) t -> p j t", j=4) for z in range(2)]
        load_words(xt_c, xt_words[0].rearrange("p n t -> p (n t)"))
        load_words(wa_c, wa_words[0])
        slot = 0
        for src in (xt_scales, wa_scales, wb_scales, wq_scales, ws_scales):
            passes = src.shape[0]
            nc.scalar.dma_start(
                out=staged[4:P:8, slot : slot + passes, :].bitcast(I32),
                in_=src.rearrange("z q c -> q z c").bitcast(I32),
            )
            slot = slot + passes
        nc.scalar.dma_start(out=raw0[:], in_=rows[0])
        nc.scalar.activation(out=half[:], in_=zero[:], func=ACT.Sigmoid)
        nc.vector.tensor_scalar(out=tiny[:], in0=half[:], scalar1=2.0 * TINY, scalar2=None, op0=ALU.mult)
        staged_flat = staged[:].rearrange("p z c -> p (z c)").bitcast(I32)

        def place(flat, lo, hi):
            words = slice(lo * N // 4, hi * N // 4)
            for r in range(4):
                nc.sync.dma_start(out=flat[r:P:32, :], in_=staged_flat[4 + 8 * r : P : 32, words])

        place(early_flat, 0, 4)
        load_words(wb_c, wb_words[0].rearrange("p n t -> p (n t)"))
        load_words(wq_c[0], wq_words[0])
        nc.sync.dma_start(out=raw1[0][:], in_=rows[1][:, :, 0:HALF])
        nc.sync.dma_start(out=raw1[1][:], in_=rows[1][:, :, HALF:T])
        load_words(wq_c[1], wq_words[1])
        place(late_flat, 4, 7)
        load_words(ws_c, ws_words.rearrange("z p c -> p z c"))

        def views(src, s0, dst, d0, n):
            return (
                dst[:, d0 : d0 + n, :].rearrange("p (c i) j -> p c j i", i=4),
                src[:, :, s0 : s0 + n].rearrange("p j (c i) -> p c j i", i=4),
            )

        def cast_v(src, s0, dst, d0, n):
            o, i = views(src, s0, dst, d0, n)
            nc.vector.tensor_copy(out=o, in_=i)

        def cast_s(src, s0, dst, d0, n):
            o, i = views(src, s0, dst, d0, n)
            nc.scalar.copy(out=o, in_=i)

        def quantize(z, h):
            cols = slice(HALF * h, HALF * (h + 1))
            nc.vector.quantize_mx(
                out=xq_c[z][:, cols].bitcast(FP8X4),
                scales=xq_s[z][:, cols],
                in_=grouped[z][h][:].rearrange("p t j -> p (t j)"),
            )

        cast_v(raw0, 0, grouped[0][0], 0, HALF)
        cast_s(raw0, HALF + 64, grouped[0][1], 64, HALF - 64)
        cast_v(raw0, HALF, grouped[0][1], 0, 64)
        quantize(0, 0)
        quantize(0, 1)
        for h in range(2):
            cast_v(raw1[h], 0, grouped[1][h], 0, 160)
            cast_s(raw1[h], 160, grouped[1][h], 160, HALF - 160)
            quantize(1, h)

        def mm(acc, w_c, fp4, w_s, j, x_c, x_s, start, stop):
            if fp4:
                lhsT = w_c[:, 2 * P * j : 2 * P * (j + 1)].bitcast(FP4X4)
            else:
                lhsT = w_c[:, P * j : P * (j + 1)].bitcast(FP8X4)
            nc.tensor.matmul_mx(
                out=acc[:], lhsT=lhsT, lhsT_scale=w_s[:, P * j : P * (j + 1)],
                rhs=x_c[:].bitcast(FP8X4), rhs_scale=x_s, start=start, stop=stop,
            )

        for w in range(WARM):
            nc.tensor.matmul_mx(
                out=r_ps[3][:, 0:P], lhsT=warm_c[:].bitcast(FP8X4), lhsT_scale=warm_s[:],
                rhs=xt_c[:, 0:P].bitcast(FP8X4), rhs_scale=warm_s[:], start=True, stop=True,
            )
        for j in range(TILES):
            mm(p_ps[j], wa_c[:], True, wa_s, j, xt_c, xt_s, True, False)
        for j in range(TILES):
            mm(r_ps[j], wb_c[:], False, wb_s, j, xt_c, xt_s, True, False)
        for j in range(TILES):
            mm(p_ps[j], wq_c[0][:], True, wq_s[0], j, xq_c[0], xq_s[0][:], False, False)
        for j in range(TILES):
            mm(p_ps[j], wq_c[1][:], True, wq_s[1], j, xq_c[1], xq_s[1][:], False, True)
        for j in range(TILES):
            mm(r_ps[j], ws_c[:, 0, :], True, ws_s[0], j, xq_c[0], xq_s[0][:], False, False)
            mm(r_ps[j], ws_c[:, 1, :], True, ws_s[1], j, xq_c[1], xq_s[1][:], False, True)

        for j in range(0, TILES, 2):
            nc.vector.tensor_copy(out=p_sb[j][:], in_=p_ps[j][:])
            nc.scalar.copy(out=p_sb[j + 1][:], in_=p_ps[j + 1][:])

        for j in range(TILES):
            for h in range(2):
                cols = slice(HALF * h, HALF * (h + 1))
                nc.vector.tensor_tensor(out=gap[j][:, cols], in0=p_sb[j][:, cols], in1=r_ps[j][:, cols], op=ALU.subtract)
                nc.scalar.activation(out=sig[j][:, cols], in_=gap[j][:, cols], func=ACT.Sigmoid)
        for j in range(TILES):
            nc.vector.scalar_tensor_tensor(
                out=base[j][:], in0=r_ps[j][:], scalar=-GAP_LIMIT, in1=p_sb[j][:], op0=ALU.add, op1=ALU.max
            )

        cuts = [[[0, 128], [128, HALF, T]], [[0, HALF, T]], [[0, HALF, T]], [[0, HALF, 384], [384, T]]]
        for j in range(TILES):
            for store in cuts[j]:
                for a, b in zip(store, store[1:]):
                    nc.scalar.activation(out=lg[j][:, a:b], in_=sig[j][:, a:b], func=ACT.Ln, bias=tiny[:])
                    nc.vector.scalar_tensor_tensor(
                        out=res[j][:, a:b], in0=lg[j][:, a:b], scalar=LOG_FLOOR, in1=base[j][:, a:b],
                        op0=ALU.max, op1=ALU.subtract, reverse1=True,
                    )
                a, b = store[0], store[-1]
                nc.sync.dma_start(out=out[P * j : P * (j + 1), a:b], in_=res[j][:, a:b])
